import numpy as np
import ml_dtypes


def mxq(x, axis, fmt="e4m3"):
    dtype, down = {"e4m3": (ml_dtypes.float8_e4m3fn, 7), "e5m2": (ml_dtypes.float8_e5m2, 14)}[fmt]
    v = np.moveaxis(np.asarray(x, np.float32).astype(ml_dtypes.bfloat16).astype(np.float64), axis, -1)
    blocks = v.reshape(v.shape[:-1] + (-1, 32))
    amax = np.abs(blocks).max(-1, keepdims=True)
    byte = np.maximum(np.where(amax > 0, np.frexp(amax)[1] - 1 + 127, 0) - down, 1)
    scale = np.exp2(byte - 127.0)
    codes = (blocks / scale).astype(np.float32).astype(dtype).astype(np.float64)
    return np.moveaxis((codes * scale).reshape(v.shape), -1, axis)


WIDE = False


def mx_kscale(k):
    if not WIDE:
        return np.ones(k)
    levels = np.array([10, -10, 5, -5, 0])
    if k % 512:
        return np.exp2(np.random.permutation(np.resize(levels, k // 32))).repeat(32)
    a = np.empty((k // 512, 16))
    for p in range(k // 512):
        a[p, :8] = np.random.permutation(np.resize(levels, 8))
        for g in range(8):
            far = levels[np.abs(levels - a[p, g]) >= 10]
            a[p, g + 8] = far[np.random.randint(len(far))]
    return np.exp2(a.ravel()).repeat(32)


def f64(x):
    return np.asarray(x).astype(np.float64)


def striped(idx):
    return np.tile(np.asarray(idx).reshape(-1, 16).T, (8, 1)).astype(np.uint16)


def unstriped(offs):
    return offs[:16].T.reshape(-1).astype(np.int64)


E2M1 = np.array([0.0, 0.5, 1.0, 1.5, 2.0, 3.0, 4.0, 6.0, -0.0, -0.5, -1.0, -1.5, -2.0, -3.0, -4.0, -6.0])


def pack_weight(w, fmt):
    k, n = w.shape
    w = f64(np.asarray(w, np.float32).astype(ml_dtypes.bfloat16)).reshape(k // 32, 32, n)
    amax = np.abs(w).max(1)
    if fmt == "e4m3":
        byte = np.frexp(amax)[1] - 1 + 127 - 7
    else:
        mant, ex = np.frexp(amax / 6.0)
        byte = np.where(mant > 0.5, ex, ex - 1) + 127
    byte = np.clip(np.where(amax > 0, byte, 1), 1, 254)
    scaled = (w * np.exp2(127.0 - byte)[:, None, :]).reshape(k, n).astype(np.float32)
    by_word = np.ascontiguousarray(scaled.reshape(k // 512, 128, 4, n).transpose(0, 1, 3, 2))
    if fmt == "e4m3":
        words = by_word.astype(ml_dtypes.float8_e4m3fn).view(np.uint8)
    else:
        c = by_word.astype(ml_dtypes.float4_e2m1fn).view(np.uint8) & 0xF
        words = (c[..., 0::2] | (c[..., 1::2] << 4)).reshape(k // 512, 128, 2 * n)
    return np.ascontiguousarray(words), np.ascontiguousarray(byte.astype(np.uint8).reshape(k // 512, 16, n))


def unpack_weight(words, scales, fmt):
    g, _, n = scales.shape
    words = np.ascontiguousarray(words).reshape(g, 128, n, -1)
    if fmt == "e4m3":
        vals = words.view(ml_dtypes.float8_e4m3fn).astype(np.float64)
    else:
        nib = np.empty((g, 128, n, 4), np.uint8)
        nib[..., 0::2] = words & 0xF
        nib[..., 1::2] = words >> 4
        vals = E2M1[nib]
    vals = vals * np.repeat(np.exp2(scales.astype(np.float64) - 127.0), 8, axis=1)[..., None]
    return vals.transpose(0, 1, 3, 2).reshape(g * 512, n)


def sigmoid(v):
    return 1.0 / (1.0 + np.exp(-v))


def bf(x):
    return np.asarray(x, np.float32).astype(ml_dtypes.bfloat16)


def planes(Y):
    r, m = Y.shape
    b = f64(bf(Y)).reshape(r // 32, 32, m)
    amax = np.abs(b).max(1)
    byte = np.clip(np.where(amax > 0, np.frexp(amax)[1] - 1 + 127 - 7, 1), 1, 254)
    codes = (b * np.exp2(127.0 - byte)[:, None, :]).reshape(r, m).astype(np.float32).astype(ml_dtypes.float8_e4m3fn).view(np.uint8)
    words = codes.reshape(r // 512, 128, 4, m).transpose(0, 1, 3, 2)
    return np.ascontiguousarray(words), np.ascontiguousarray(byte.astype(np.uint8).reshape(r // 512, 16, m))


D, T, I, Q, E, Z, M, C = 512, 2048, 512, 256, 512, 1024, 1024, 512


def setup_inputs():
    n = np.random.standard_normal
    idx = np.random.permutation(T)[:I]
    idx2 = np.random.permutation(Z)[:I]
    idx3 = np.random.permutation(Z)[:I]
    idx4 = np.random.permutation(M)[:Q]
    fd = mx_kscale(D)
    fi = mx_kscale(I)
    fc = mx_kscale(C)
    ti = np.ones(T)
    ti[idx] = fi
    keysp = pack_weight(n((D, T)) / fd[:, None], "e2m1")
    return {
        "query": (n((D, Q)) * 1.0 / np.sqrt(D) * fd[:, None]).astype(np.float32),
        "query2": (n((D, Q)) * 1.0 / np.sqrt(D) * fd[:, None]).astype(np.float32),
        "keys_words": keysp[0],
        "keys_scales": keysp[1],
        "pages": (n((D, Z)) / fd[:, None]).astype(np.float32),
        "os": (np.random.uniform(0.02, 0.08, (1, I)) * fi).astype(np.float32),
        "vals": (n((E, T)) / ti).astype(np.float32),
        "wm": (n((C, E)) * 1.0 / np.sqrt(C) * fc[:, None]).astype(np.float32),
        "mstore": (n((C, M)) / fc[:, None]).astype(np.float32),
        "offs": striped(idx),
        "offs2": striped(idx2),
        "offs3": striped(idx3),
        "offs4": striped(idx4),
    }


def reference(query, query2, keys_words, keys_scales, pages, os, vals, wm, mstore, offs, offs2, offs3, offs4):
    idx = unstriped(offs)
    idx2 = unstriped(offs2)
    idx3 = unstriped(offs3)
    idx4 = unstriped(offs4)
    keysu = unpack_weight(keys_words, keys_scales, "e2m1")
    queryq = mxq(f64(query), 0, "e4m3")
    a = queryq.T @ keysu
    query2q = mxq(f64(query2), 0, "e4m3")
    pagesq = mxq(f64(pages), 0, "e4m3")
    h0 = query2q.T @ pagesq
    s = np.maximum(a[:, idx], h0[:, idx2]) - h0[:, idx3]
    w = sigmoid(s)
    wo1 = w * f64(os)
    wt1 = wo1.T
    vt1 = f64(vals)[:, idx].T
    vt1q = mxq(vt1, 0, "e4m3")
    wt1q = mxq(wt1, 0, "e4m3")
    wmq = mxq(f64(wm), 0, "e4m3")
    mstoreidx4q = mxq(f64(mstore)[:, idx4], 0, "e4m3")
    o = vt1q.T @ wt1q + wmq.T @ mstoreidx4q
    words, scales = planes(o)
    return o, words, scales

@@ -1,0 +1,244 @@
+from contextlib import ExitStack
+
+import concourse.mybir as mybir
+from concourse.masks import make_identity
+
+D, T, I, Q, E, Z, M, C = 512, 2048, 512, 256, 512, 1024, 1024, 512
+FLOPS = 2 * Q * (D * T + D * Z + I * E + C * E)
+
+F32 = mybir.dt.float32
+BF16 = mybir.dt.bfloat16
+I32 = mybir.dt.int32
+U32 = mybir.dt.uint32
+U16 = mybir.dt.uint16
+U8 = mybir.dt.uint8
+FP8X4 = mybir.dt.float8_e4m3fn_x4
+FP4X4 = mybir.dt.float4_e2m1fn_x4
+ALU = mybir.AluOpType
+ACT = mybir.ActivationFunctionType
+
+P = 128
+PACK = 4
+BANK = 512
+HALVES = Q // P
+
+
+def tile_attend_largestof3_addedmemory_lean_pl_kernel(
+    tc, query, query2, keys_words, keys_scales, pages, slot_scale, vals, wm, mstore, offs, offs2, offs3, offs4, out_0, out_1, out_2
+):
+    nc = tc.nc
+    with ExitStack() as ctx:
+        keep = ctx.enter_context(tc.tile_pool(name="keep", bufs=1))
+        scores_psum = ctx.enter_context(tc.psum_pool(name="scores_psum", bufs=4))
+        turn_psum = ctx.enter_context(tc.psum_pool(name="turn_psum", bufs=2))
+        out_psum = ctx.enter_context(tc.psum_pool(name="out_psum", bufs=1))
+
+        def sbuf(name, shape, dtype, after=None):
+            return keep.tile(shape, dtype, name=name, tag=after or name, align_bytes=64)
+
+        def by_four(rows):
+            return rows.rearrange("(p j) w -> p j w", j=PACK)
+
+        def load(name, shape, dtype, source):
+            tile = sbuf(name, shape, dtype)
+            nc.sync.dma_start(tile[:], source)
+            return tile
+
+        def quantise(name, grouped, words):
+            codes = sbuf(name + "_codes", [P, words], U32)
+            scales = sbuf(name + "_scales", [P, words], U8)
+            nc.vector.quantize_mx(out=codes[:].bitcast(FP8X4), scales=scales[:], in_=grouped)
+            return codes, scales
+
+        def interleave(name, raw, width):
+            grouped = sbuf(name + "_grouped", [P, width * PACK], BF16)
+            nc.vector.tensor_copy(
+                out=grouped[:].rearrange("p (c i t) -> p c t i", i=4, t=PACK),
+                in_=raw.rearrange("p t (c i) -> p c t i", i=4),
+            )
+            return grouped
+
+        def scalar_copy(out, in_):
+            nc.scalar.activation(out, in_, ACT.Copy)
+
+        def vector_copy(out, in_):
+            nc.vector.tensor_copy(out=out, in_=in_)
+
+        key_scales = sbuf("key_scales", [P, T], U8)
+        nc.vector.memset(key_scales[:].bitcast(I32), 0)
+        query_raw = load("query_raw", [P, PACK, Q], F32, by_four(query))
+        for quad in range(4):
+            nc.sync.dma_start(
+                key_scales[32 * quad : 32 * quad + 4, :].bitcast(I32),
+                keys_scales[0, 4 * quad : 4 * quad + 4, :].bitcast(I32),
+            )
+        key_words = sbuf("key_words", [P, 2 * T], U8)
+        nc.sync.dma_start(key_words[:].bitcast(I32), keys_words[0].bitcast(I32))
+        token_list = load("token_list", [P, I // 16], U16, offs)
+        query2_raw = load("query2_raw", [P, PACK, Q], F32, by_four(query2))
+        pages_raw = [
+            load("pages_raw%d" % n, [P, PACK, BANK], F32, by_four(pages)[:, :, n * BANK : (n + 1) * BANK])
+            for n in range(Z // BANK)
+        ]
+        page_list = load("page_list", [P, I // 16], U16, offs2)
+        base_list = load("base_list", [P, I // 16], U16, offs3)
+        memory_list = load("memory_list", [P, Q // 16], U16, offs4)
+        slot_factor = load("slot_factor", [P, PACK], F32, slot_scale.rearrange("o (p t) -> p (o t)", t=PACK))
+        mstore_raw = [load("mstore_raw%d" % j, [P, M], F32, by_four(mstore)[:, j, :]) for j in range(PACK)]
+        wm_raw = load("wm_raw", [P, PACK, E], F32, by_four(wm))
+        vals_raw = [load("vals_raw%d" % j, [P, T], F32, by_four(vals)[:, j, :]) for j in range(PACK)]
+
+        identity = sbuf("identity", [P, P], F32)
+        make_identity(nc, identity[:])
+
+        query_mx = []
+        for h in range(HALVES):
+            grouped = interleave("query%d" % h, query_raw[:, :, h * P : (h + 1) * P], P)
+            query_mx.append(quantise("query%d" % h, grouped[:], P))
+        token_scores = []
+        for h in range(HALVES):
+            codes, scales = query_mx[h]
+            whole = sbuf("a%d" % h, [P, T], F32)
+            for n in range(T // BANK):
+                bank = scores_psum.tile([P, BANK], F32, name="scores")
+                nc.tensor.matmul_mx(
+                    out=bank[:],
+                    lhsT=codes[:].bitcast(FP8X4),
+                    lhsT_scale=scales[:],
+                    rhs=key_words[:, 2 * n * BANK : 2 * (n + 1) * BANK].bitcast(FP4X4),
+                    rhs_scale=key_scales[:, n * BANK : (n + 1) * BANK],
+                    start=True,
+                    stop=True,
+                )
+                copy = vector_copy if (4 * h + n) in (1, 3) else scalar_copy
+                copy(whole[:, n * BANK : (n + 1) * BANK], bank[:])
+            picked = sbuf("a_picked%d" % h, [P, I], F32)
+            scalar_copy(picked[:], whole[:].indirect(token_list[:]))
+            token_scores.append(picked)
+
+        query2_codes, query2_scales = quantise("query2", interleave("query2", query2_raw[:], Q)[:], Q)
+        page_scores = [sbuf("h0_%d" % h, [P, Z], F32) for h in range(HALVES)]
+        for n in range(Z // BANK):
+            codes, scales = quantise("pages%d" % n, interleave("pages%d" % n, pages_raw[n][:], BANK)[:], BANK)
+            for h in range(HALVES):
+                bank = scores_psum.tile([P, BANK], F32, name="scores")
+                nc.tensor.matmul_mx(
+                    out=bank[:],
+                    lhsT=query2_codes[:, h * P : (h + 1) * P].bitcast(FP8X4),
+                    lhsT_scale=query2_scales[:, h * P : (h + 1) * P],
+                    rhs=codes[:].bitcast(FP8X4),
+                    rhs_scale=scales[:],
+                    start=True,
+                    stop=True,
+                )
+                copy = vector_copy if (n, h) == (1, 0) else scalar_copy
+                copy(page_scores[h][:, n * BANK : (n + 1) * BANK], bank[:])
+
+        weights_mx = []
+        for h in range(HALVES):
+            page_picked = sbuf("h0_picked%d" % h, [P, I], F32)
+            copy = vector_copy if h == 0 else scalar_copy
+            copy(page_picked[:], page_scores[h][:].indirect(page_list[:]))
+            larger = sbuf("larger%d" % h, [P, I], F32)
+            nc.vector.tensor_tensor(larger[:], token_scores[h][:], page_picked[:], ALU.max)
+            minus_s = sbuf("minus_s%d" % h, [P, I], F32)
+            nc.vector.tensor_tensor(minus_s[:], page_scores[h][:].indirect(base_list[:]), larger[:], ALU.subtract)
+            weights = sbuf("weights%d" % h, [P, I], F32)
+            nc.scalar.activation(weights[:], minus_s[:], ACT.Sigmoid, scale=-1.0)
+            turned = turn_psum.tile([P, PACK, P], F32, name="turned")
+            for t in range(PACK):
+                nc.tensor.transpose(turned[:, t, :], weights[:, t::PACK], identity[:])
+            grouped = sbuf("weights_grouped%d" % h, [P, P, PACK], BF16)
+            nc.vector.tensor_tensor(
+                grouped[:],
+                turned[:].rearrange("p t q -> p q t"),
+                slot_factor[:].unsqueeze(1).to_broadcast([P, P, PACK]),
+                ALU.mult,
+            )
+            weights_mx.append(quantise("weights%d" % h, grouped[:].rearrange("p q t -> p (q t)"), P))
+
+        clock = sbuf("clock", [P, 8], BF16)
+        nc.gpsimd.tensor_copy(clock[:, 0:1], larger[:, 0:1])
+        memory_picked = sbuf("memory_picked", [P, PACK, Q], BF16, after="pages1_grouped")
+        for j in range(PACK):
+            copy = vector_copy if j < 2 else scalar_copy
+            copy(memory_picked[:, j, :], mstore_raw[j][:].indirect(memory_list[:]))
+        memory_codes, memory_scales = quantise("memory", interleave("memory", memory_picked[:], Q)[:], Q)
+        wm_grouped = sbuf("wm_grouped", [P, E * PACK], BF16, after="larger1")
+        nc.vector.tensor_copy(
+            out=wm_grouped[:].rearrange("p (t m j) -> p m j t", t=PACK, j=PACK),
+            in_=wm_raw[:].rearrange("p j (m t) -> p m j t", t=PACK),
+        )
+        wm_codes, wm_scales = quantise("wm", wm_grouped[:], E)
+
+        result = [out_psum.tile([P, PACK, P], F32, name="result%d" % h) for h in range(HALVES)]
+        out_rows = by_four(out_0)
+        early = sbuf("early", [P, PACK - 1, Q], F32)
+        last = sbuf("last", [P, Q], F32)
+        for t in range(PACK):
+            for h in range(HALVES):
+                nc.tensor.matmul_mx(
+                    out=result[h][:, t, :],
+                    lhsT=wm_codes[:, t * P : (t + 1) * P].bitcast(FP8X4),
+                    lhsT_scale=wm_scales[:, t * P : (t + 1) * P],
+                    rhs=memory_codes[:, h * P : (h + 1) * P].bitcast(FP8X4),
+                    rhs_scale=memory_scales[:, h * P : (h + 1) * P],
+                    start=True,
+                    stop=False,
+                )
+            picked = sbuf("vals_picked%d" % t, [P, I], BF16, after="minus_s1" if t == 0 else None)
+            if t < PACK - 1:
+                scalar_copy(picked[:], vals_raw[t][:].indirect(token_list[:]))
+            else:
+                vector_copy(picked[:, : I // 2], vals_raw[t][:].indirect(token_list[:, : I // 32]))
+                scalar_copy(picked[:, I // 2 :], vals_raw[t][:].indirect(token_list[:, I // 32 :]))
+            pairs = picked[:].bitcast(F32)
+            turned = turn_psum.tile([P, PACK, P], F32, name="turned")
+            for u in range(2):
+                nc.tensor.transpose(turned[:, u, :], pairs[:, u::2], identity[:])
+            grouped = sbuf("vals_grouped%d" % t, [P, P * PACK], BF16)
+            move = vector_copy
+            move(
+                grouped[:].bitcast(F32).rearrange("p (e u) -> p e u", u=2),
+                turned[:, 0:2, :].rearrange("p u e -> p e u"),
+            )
+            codes, scales = quantise("vals%d" % t, grouped[:], P)
+            if t == 0:
+                nc.gpsimd.tensor_copy(clock[:, 2:3], grouped[:, 0:1])
+            for h in range(HALVES):
+                weight_codes, weight_scales = weights_mx[h]
+                nc.tensor.matmul_mx(
+                    out=result[h][:, t, :],
+                    lhsT=codes[:].bitcast(FP8X4),
+                    lhsT_scale=scales[:],
+                    rhs=weight_codes[:].bitcast(FP8X4),
+                    rhs_scale=weight_scales[:],
+                    start=False,
+                    stop=True,
+                )
+            if t == PACK - 2:
+                for h in range(HALVES):
+                    scalar_copy(early[:, :, h * P : (h + 1) * P], result[h][:, 0 : PACK - 1, :])
+                nc.sync.dma_start(out_rows[:, 0 : PACK - 1, :], early[:])
+
+        out_codes = sbuf("out_codes", [P, Q], U32)
+        out_scales = sbuf("out_scales", [P, Q], U8)
+        out_grouped = [sbuf("out_grouped%d" % h, [P, P, PACK], BF16) for h in range(HALVES)]
+        vector_copy(out_grouped[0][:], result[0][:].rearrange("p t q -> p q t"))
+        scalar_copy(out_grouped[1][:], result[1][:].rearrange("p t q -> p q t"))
+        for h in reversed(range(HALVES)):
+            scalar_copy(last[:, h * P : (h + 1) * P], result[h][:, PACK - 1, :])
+        nc.scalar.dma_start(out_rows[:, PACK - 1, :], last[:])
+        for h in range(HALVES):
+            nc.vector.quantize_mx(
+                out=out_codes[:, h * P : (h + 1) * P].bitcast(FP8X4),
+                scales=out_scales[:, h * P : (h + 1) * P],
+                in_=out_grouped[h][:].rearrange("p q t -> p (q t)"),
+            )
+        nc.sync.dma_start(out_1[0].rearrange("p c r -> p (c r)").bitcast(I32), out_codes[:].bitcast(I32))
+        for quad in range(4):
+            queue = nc.sync if quad < 2 else nc.scalar
+            queue.dma_start(
+                out_2[0, 4 * quad : 4 * quad + 4, :].bitcast(I32),
+                out_scales[32 * quad : 32 * quad + 4, :].bitcast(I32),
+            )

@@ -30,8 +30,7 @@ def tile_attend_largestof3_addedmemory_lean_pl_kernel(
     with ExitStack() as ctx:
         keep = ctx.enter_context(tc.tile_pool(name="keep", bufs=1))
         scores_psum = ctx.enter_context(tc.psum_pool(name="scores_psum", bufs=4))
-        turn_psum = ctx.enter_context(tc.psum_pool(name="turn_psum", bufs=2))
-        out_psum = ctx.enter_context(tc.psum_pool(name="out_psum", bufs=1))
+        turn_psum = ctx.enter_context(tc.psum_pool(name="turn_psum", bufs=4))
 
         def sbuf(name, shape, dtype, after=None):
             return keep.tile(shape, dtype, name=name, tag=after or name, align_bytes=64)
@@ -44,14 +43,14 @@ def tile_attend_largestof3_addedmemory_lean_pl_kernel(
             nc.sync.dma_start(tile[:], source)
             return tile
 
-        def quantise(name, grouped, words):
-            codes = sbuf(name + "_codes", [P, words], U32)
+        def quantise(name, grouped, words, after=None):
+            codes = sbuf(name + "_codes", [P, words], U32, after=after)
             scales = sbuf(name + "_scales", [P, words], U8)
             nc.vector.quantize_mx(out=codes[:].bitcast(FP8X4), scales=scales[:], in_=grouped)
             return codes, scales
 
-        def interleave(name, raw, width):
-            grouped = sbuf(name + "_grouped", [P, width * PACK], BF16)
+        def interleave(name, raw, width, after=None):
+            grouped = sbuf(name + "_grouped", [P, width * PACK], BF16, after=after)
             nc.vector.tensor_copy(
                 out=grouped[:].rearrange("p (c i t) -> p c t i", i=4, t=PACK),
                 in_=raw.rearrange("p t (c i) -> p c t i", i=4),
@@ -72,8 +71,9 @@ def tile_attend_largestof3_addedmemory_lean_pl_kernel(
                 key_scales[32 * quad : 32 * quad + 4, :].bitcast(I32),
                 keys_scales[0, 4 * quad : 4 * quad + 4, :].bitcast(I32),
             )
-        key_words = sbuf("key_words", [P, 2 * T], U8)
-        nc.sync.dma_start(key_words[:].bitcast(I32), keys_words[0].bitcast(I32))
+        key_words = [sbuf("key_words%d" % n, [P, T], U8) for n in range(2)]
+        for n in range(2):
+            nc.sync.dma_start(key_words[n][:].bitcast(I32), keys_words[0, :, n * T : (n + 1) * T].bitcast(I32))
         token_list = load("token_list", [P, I // 16], U16, offs)
         query2_raw = load("query2_raw", [P, PACK, Q], F32, by_four(query2))
         pages_raw = [
@@ -84,8 +84,8 @@ def tile_attend_largestof3_addedmemory_lean_pl_kernel(
         base_list = load("base_list", [P, I // 16], U16, offs3)
         memory_list = load("memory_list", [P, Q // 16], U16, offs4)
         slot_factor = load("slot_factor", [P, PACK], F32, slot_scale.rearrange("o (p t) -> p (o t)", t=PACK))
-        mstore_raw = [load("mstore_raw%d" % j, [P, M], F32, by_four(mstore)[:, j, :]) for j in range(PACK)]
         wm_raw = load("wm_raw", [P, PACK, E], F32, by_four(wm))
+        mstore_raw = [load("mstore_raw%d" % j, [P, M], F32, by_four(mstore)[:, j, :]) for j in range(PACK)]
         vals_raw = [load("vals_raw%d" % j, [P, T], F32, by_four(vals)[:, j, :]) for j in range(PACK)]
 
         identity = sbuf("identity", [P, P], F32)
@@ -100,17 +100,17 @@ def tile_attend_largestof3_addedmemory_lean_pl_kernel(
             codes, scales = query_mx[h]
             whole = sbuf("a%d" % h, [P, T], F32)
             for n in range(T // BANK):
-                bank = scores_psum.tile([P, BANK], F32, name="scores")
+                bank = scores_psum.tile([P, BANK], F32, name="scores", tag="scores")
                 nc.tensor.matmul_mx(
                     out=bank[:],
                     lhsT=codes[:].bitcast(FP8X4),
                     lhsT_scale=scales[:],
-                    rhs=key_words[:, 2 * n * BANK : 2 * (n + 1) * BANK].bitcast(FP4X4),
+                    rhs=key_words[n // 2][:, 2 * (n % 2) * BANK : 2 * (n % 2 + 1) * BANK].bitcast(FP4X4),
                     rhs_scale=key_scales[:, n * BANK : (n + 1) * BANK],
                     start=True,
                     stop=True,
                 )
-                copy = vector_copy if (4 * h + n) in (1, 3) else scalar_copy
+                copy = vector_copy if (4 * h + n) in (1, 3, 5) else scalar_copy
                 copy(whole[:, n * BANK : (n + 1) * BANK], bank[:])
             picked = sbuf("a_picked%d" % h, [P, I], F32)
             scalar_copy(picked[:], whole[:].indirect(token_list[:]))
@@ -119,9 +119,10 @@ def tile_attend_largestof3_addedmemory_lean_pl_kernel(
         query2_codes, query2_scales = quantise("query2", interleave("query2", query2_raw[:], Q)[:], Q)
         page_scores = [sbuf("h0_%d" % h, [P, Z], F32) for h in range(HALVES)]
         for n in range(Z // BANK):
-            codes, scales = quantise("pages%d" % n, interleave("pages%d" % n, pages_raw[n][:], BANK)[:], BANK)
+            grouped = interleave("pages%d" % n, pages_raw[n][:], BANK)
+            codes, scales = quantise("pages%d" % n, grouped[:], BANK)
             for h in range(HALVES):
-                bank = scores_psum.tile([P, BANK], F32, name="scores")
+                bank = scores_psum.tile([P, BANK], F32, name="scores", tag="scores")
                 nc.tensor.matmul_mx(
                     out=bank[:],
                     lhsT=query2_codes[:, h * P : (h + 1) * P].bitcast(FP8X4),
@@ -131,62 +132,65 @@ def tile_attend_largestof3_addedmemory_lean_pl_kernel(
                     start=True,
                     stop=True,
                 )
-                copy = vector_copy if (n, h) == (1, 0) else scalar_copy
-                copy(page_scores[h][:, n * BANK : (n + 1) * BANK], bank[:])
+                scalar_copy(page_scores[h][:, n * BANK : (n + 1) * BANK], bank[:])
 
-        weights_mx = []
+        page_picked = [sbuf("h0_picked%d" % h, [P, I], F32) for h in range(HALVES)]
         for h in range(HALVES):
-            page_picked = sbuf("h0_picked%d" % h, [P, I], F32)
-            copy = vector_copy if h == 0 else scalar_copy
-            copy(page_picked[:], page_scores[h][:].indirect(page_list[:]))
-            larger = sbuf("larger%d" % h, [P, I], F32)
-            nc.vector.tensor_tensor(larger[:], token_scores[h][:], page_picked[:], ALU.max)
-            minus_s = sbuf("minus_s%d" % h, [P, I], F32)
-            nc.vector.tensor_tensor(minus_s[:], page_scores[h][:].indirect(base_list[:]), larger[:], ALU.subtract)
-            weights = sbuf("weights%d" % h, [P, I], F32)
-            nc.scalar.activation(weights[:], minus_s[:], ACT.Sigmoid, scale=-1.0)
-            turned = turn_psum.tile([P, PACK, P], F32, name="turned")
-            for t in range(PACK):
-                nc.tensor.transpose(turned[:, t, :], weights[:, t::PACK], identity[:])
-            grouped = sbuf("weights_grouped%d" % h, [P, P, PACK], BF16)
-            nc.vector.tensor_tensor(
-                grouped[:],
-                turned[:].rearrange("p t q -> p q t"),
-                slot_factor[:].unsqueeze(1).to_broadcast([P, P, PACK]),
-                ALU.mult,
-            )
-            weights_mx.append(quantise("weights%d" % h, grouped[:].rearrange("p q t -> p (q t)"), P))
-
-        clock = sbuf("clock", [P, 8], BF16)
-        nc.gpsimd.tensor_copy(clock[:, 0:1], larger[:, 0:1])
-        memory_picked = sbuf("memory_picked", [P, PACK, Q], BF16, after="pages1_grouped")
+            scalar_copy(page_picked[h][:], page_scores[h][:].indirect(page_list[:]))
+        memory_picked = sbuf("memory_picked", [P, PACK, Q], BF16, after="pages1_codes")
         for j in range(PACK):
-            copy = vector_copy if j < 2 else scalar_copy
-            copy(memory_picked[:, j, :], mstore_raw[j][:].indirect(memory_list[:]))
-        memory_codes, memory_scales = quantise("memory", interleave("memory", memory_picked[:], Q)[:], Q)
-        wm_grouped = sbuf("wm_grouped", [P, E * PACK], BF16, after="larger1")
+            scalar_copy(memory_picked[:, j, :], mstore_raw[j][:].indirect(memory_list[:]))
+        wm_grouped = sbuf("wm_grouped", [P, E * PACK], BF16, after="pages1_grouped")
         nc.vector.tensor_copy(
             out=wm_grouped[:].rearrange("p (t m j) -> p m j t", t=PACK, j=PACK),
             in_=wm_raw[:].rearrange("p j (m t) -> p m j t", t=PACK),
         )
         wm_codes, wm_scales = quantise("wm", wm_grouped[:], E)
-
-        result = [out_psum.tile([P, PACK, P], F32, name="result%d" % h) for h in range(HALVES)]
-        out_rows = by_four(out_0)
-        early = sbuf("early", [P, PACK - 1, Q], F32)
-        last = sbuf("last", [P, Q], F32)
+        minus_s = []
+        for h in range(HALVES):
+            larger = sbuf("larger%d" % h, [P, I], F32, after="larger")
+            nc.vector.tensor_tensor(larger[:], token_scores[h][:], page_picked[h][:], ALU.max)
+            minus_s.append(sbuf("minus_s%d" % h, [P, I], F32))
+            nc.vector.tensor_tensor(minus_s[h][:], page_scores[h][:].indirect(base_list[:]), larger[:], ALU.subtract)
+        memory_grouped = interleave("memory", memory_picked[:], Q, after="h0_1")
+        memory_codes, memory_scales = quantise("memory", memory_grouped[:], Q)
+        weights_grouped = sbuf("weights_grouped", [P, Q, PACK], BF16)
+        for h in range(HALVES):
+            weights = sbuf("weights%d" % h, [P, PACK, P], F32, after=("mstore_raw3", None)[h])
+            nc.scalar.activation(
+                weights[:].rearrange("p t s -> p s t"),
+                minus_s[h][:].rearrange("p (s t) -> p s t", t=PACK),
+                ACT.Sigmoid,
+                scale=-1.0,
+            )
+            turned = turn_psum.tile([P, PACK, P], F32, name="turned")
+            for t in range(PACK):
+                nc.tensor.transpose(turned[:, t, :], weights[:, t, :], identity[:])
+            nc.vector.tensor_tensor(
+                weights_grouped[:, h * P : (h + 1) * P, :],
+                turned[:].rearrange("p t q -> p q t"),
+                slot_factor[:].unsqueeze(1).to_broadcast([P, P, PACK]),
+                ALU.mult,
+            )
+        weight_codes, weight_scales = quantise("weights", weights_grouped[:].rearrange("p q t -> p (q t)"), Q)
+        result = [scores_psum.tile([P, Q], F32, name="result%d" % t, tag="scores") for t in range(PACK)]
         for t in range(PACK):
-            for h in range(HALVES):
-                nc.tensor.matmul_mx(
-                    out=result[h][:, t, :],
-                    lhsT=wm_codes[:, t * P : (t + 1) * P].bitcast(FP8X4),
-                    lhsT_scale=wm_scales[:, t * P : (t + 1) * P],
-                    rhs=memory_codes[:, h * P : (h + 1) * P].bitcast(FP8X4),
-                    rhs_scale=memory_scales[:, h * P : (h + 1) * P],
-                    start=True,
-                    stop=False,
-                )
-            picked = sbuf("vals_picked%d" % t, [P, I], BF16, after="minus_s1" if t == 0 else None)
+            nc.tensor.matmul_mx(
+                out=result[t][:],
+                lhsT=wm_codes[:, t * P : (t + 1) * P].bitcast(FP8X4),
+                lhsT_scale=wm_scales[:, t * P : (t + 1) * P],
+                rhs=memory_codes[:].bitcast(FP8X4),
+                rhs_scale=memory_scales[:],
+                start=True,
+                stop=False,
+            )
+
+        out_rows = by_four(out_0)
+        picked_after = ("minus_s0", "minus_s1", "vals_raw1", "vals_raw1")
+        codes_after = ("minus_s1", "vals_raw2", None, None)
+
+        def turn_values(t):
+            picked = sbuf("vals_picked%d" % t, [P, I], BF16, after=picked_after[t])
             if t < PACK - 1:
                 scalar_copy(picked[:], vals_raw[t][:].indirect(token_list[:]))
             else:
@@ -197,44 +201,38 @@ def tile_attend_largestof3_addedmemory_lean_pl_kernel(
             for u in range(2):
                 nc.tensor.transpose(turned[:, u, :], pairs[:, u::2], identity[:])
             grouped = sbuf("vals_grouped%d" % t, [P, P * PACK], BF16)
-            move = vector_copy
-            move(
+            vector_copy(
                 grouped[:].bitcast(F32).rearrange("p (e u) -> p e u", u=2),
                 turned[:, 0:2, :].rearrange("p u e -> p e u"),
             )
-            codes, scales = quantise("vals%d" % t, grouped[:], P)
-            if t == 0:
-                nc.gpsimd.tensor_copy(clock[:, 2:3], grouped[:, 0:1])
-            for h in range(HALVES):
-                weight_codes, weight_scales = weights_mx[h]
-                nc.tensor.matmul_mx(
-                    out=result[h][:, t, :],
-                    lhsT=codes[:].bitcast(FP8X4),
-                    lhsT_scale=scales[:],
-                    rhs=weight_codes[:].bitcast(FP8X4),
-                    rhs_scale=weight_scales[:],
-                    start=False,
-                    stop=True,
-                )
-            if t == PACK - 2:
-                for h in range(HALVES):
-                    scalar_copy(early[:, :, h * P : (h + 1) * P], result[h][:, 0 : PACK - 1, :])
-                nc.sync.dma_start(out_rows[:, 0 : PACK - 1, :], early[:])
+            return grouped
 
-        out_codes = sbuf("out_codes", [P, Q], U32)
-        out_scales = sbuf("out_scales", [P, Q], U8)
-        out_grouped = [sbuf("out_grouped%d" % h, [P, P, PACK], BF16) for h in range(HALVES)]
-        vector_copy(out_grouped[0][:], result[0][:].rearrange("p t q -> p q t"))
-        scalar_copy(out_grouped[1][:], result[1][:].rearrange("p t q -> p q t"))
-        for h in reversed(range(HALVES)):
-            scalar_copy(last[:, h * P : (h + 1) * P], result[h][:, PACK - 1, :])
-        nc.scalar.dma_start(out_rows[:, PACK - 1, :], last[:])
-        for h in range(HALVES):
-            nc.vector.quantize_mx(
-                out=out_codes[:, h * P : (h + 1) * P].bitcast(FP8X4),
-                scales=out_scales[:, h * P : (h + 1) * P],
-                in_=out_grouped[h][:].rearrange("p q t -> p (q t)"),
+        def multiply(t, grouped):
+            codes, scales = quantise("vals%d" % t, grouped[:], P, after=codes_after[t])
+            nc.tensor.matmul_mx(
+                out=result[t][:],
+                lhsT=codes[:].bitcast(FP8X4),
+                lhsT_scale=scales[:],
+                rhs=weight_codes[:].bitcast(FP8X4),
+                rhs_scale=weight_scales[:],
+                start=False,
+                stop=True,
             )
+
+        vals_grouped = [turn_values(0), turn_values(1)]
+        multiply(0, vals_grouped[0])
+        vals_grouped.append(turn_values(2))
+        multiply(1, vals_grouped[1])
+        vals_grouped.append(turn_values(3))
+        multiply(2, vals_grouped[2])
+        finished = sbuf("finished", [P, PACK, Q], F32, after="vals_raw3")
+        for t in range(PACK - 1):
+            scalar_copy(finished[:, t, :], result[t][:])
+        nc.sync.dma_start(out_rows[:, : PACK - 1, :], finished[:, : PACK - 1, :])
+        multiply(3, vals_grouped[3])
+        scalar_copy(finished[:, PACK - 1, :], result[PACK - 1][:])
+        nc.scalar.dma_start(out_rows[:, PACK - 1, :], finished[:, PACK - 1, :])
+        out_codes, out_scales = quantise("out", interleave("out", finished[:], Q)[:], Q)
         nc.sync.dma_start(out_1[0].rearrange("p c r -> p (c r)").bitcast(I32), out_codes[:].bitcast(I32))
         for quad in range(4):
             queue = nc.sync if quad < 2 else nc.scalar

@@ -49,8 +49,8 @@ def tile_attend_largestof3_addedmemory_lean_pl_kernel(
             nc.vector.quantize_mx(out=codes[:].bitcast(FP8X4), scales=scales[:], in_=grouped)
             return codes, scales
 
-        def interleave(name, raw, width, after=None):
-            grouped = sbuf(name + "_grouped", [P, width * PACK], BF16, after=after)
+        def interleave(name, raw, width):
+            grouped = sbuf(name + "_grouped", [P, width * PACK], BF16)
             nc.vector.tensor_copy(
                 out=grouped[:].rearrange("p (c i t) -> p c t i", i=4, t=PACK),
                 in_=raw.rearrange("p t (c i) -> p c t i", i=4),
@@ -137,26 +137,46 @@ def tile_attend_largestof3_addedmemory_lean_pl_kernel(
         page_picked = [sbuf("h0_picked%d" % h, [P, I], F32) for h in range(HALVES)]
         for h in range(HALVES):
             scalar_copy(page_picked[h][:], page_scores[h][:].indirect(page_list[:]))
-        memory_picked = sbuf("memory_picked", [P, PACK, Q], BF16, after="pages1_codes")
-        for j in range(PACK):
-            scalar_copy(memory_picked[:, j, :], mstore_raw[j][:].indirect(memory_list[:]))
         wm_grouped = sbuf("wm_grouped", [P, E * PACK], BF16, after="pages1_grouped")
         nc.vector.tensor_copy(
             out=wm_grouped[:].rearrange("p (t m j) -> p m j t", t=PACK, j=PACK),
             in_=wm_raw[:].rearrange("p j (m t) -> p m j t", t=PACK),
         )
         wm_codes, wm_scales = quantise("wm", wm_grouped[:], E)
-        minus_s = []
-        for h in range(HALVES):
+        memory_grouped = sbuf("memory_grouped", [P, Q, PACK], BF16)
+
+        def pick_memory(pair, copy, after):
+            picked = sbuf("memory_picked%d" % pair, [P, 2, Q], BF16, after=after)
+            for j in range(2):
+                copy(picked[:, j, :], mstore_raw[2 * pair + j][:].indirect(memory_list[:]))
+            vector_copy(memory_grouped[:, :, 2 * pair : 2 * pair + 2], picked[:].rearrange("p j q -> p q j"))
+
+        def negated_scores(h, after):
             larger = sbuf("larger%d" % h, [P, I], F32, after="larger")
             nc.vector.tensor_tensor(larger[:], token_scores[h][:], page_picked[h][:], ALU.max)
-            minus_s.append(sbuf("minus_s%d" % h, [P, I], F32))
-            nc.vector.tensor_tensor(minus_s[h][:], page_scores[h][:].indirect(base_list[:]), larger[:], ALU.subtract)
-        memory_grouped = interleave("memory", memory_picked[:], Q, after="h0_1")
-        memory_codes, memory_scales = quantise("memory", memory_grouped[:], Q)
+            negated = sbuf("minus_s%d" % h, [P, I], F32, after=after)
+            nc.vector.tensor_tensor(negated[:], page_scores[h][:].indirect(base_list[:]), larger[:], ALU.subtract)
+            return negated
+
+        pick_memory(0, vector_copy, "pages1_grouped")
+        minus_s = [negated_scores(0, None)]
+        pick_memory(1, scalar_copy, "a_picked0")
+        memory_codes, memory_scales = quantise("memory", memory_grouped[:].rearrange("p q t -> p (q t)"), Q)
+        result = [scores_psum.tile([P, Q], F32, name="result%d" % t, tag="scores") for t in range(PACK)]
+        for t in range(PACK):
+            nc.tensor.matmul_mx(
+                out=result[t][:],
+                lhsT=wm_codes[:, t * P : (t + 1) * P].bitcast(FP8X4),
+                lhsT_scale=wm_scales[:, t * P : (t + 1) * P],
+                rhs=memory_codes[:].bitcast(FP8X4),
+                rhs_scale=memory_scales[:],
+                start=True,
+                stop=False,
+            )
+        minus_s.append(negated_scores(1, "memory_grouped"))
         weights_grouped = sbuf("weights_grouped", [P, Q, PACK], BF16)
         for h in range(HALVES):
-            weights = sbuf("weights%d" % h, [P, PACK, P], F32, after=("mstore_raw3", None)[h])
+            weights = sbuf("weights%d" % h, [P, PACK, P], F32)
             nc.scalar.activation(
                 weights[:].rearrange("p t s -> p s t"),
                 minus_s[h][:].rearrange("p (s t) -> p s t", t=PACK),
@@ -173,21 +193,10 @@ def tile_attend_largestof3_addedmemory_lean_pl_kernel(
                 ALU.mult,
             )
         weight_codes, weight_scales = quantise("weights", weights_grouped[:].rearrange("p q t -> p (q t)"), Q)
-        result = [scores_psum.tile([P, Q], F32, name="result%d" % t, tag="scores") for t in range(PACK)]
-        for t in range(PACK):
-            nc.tensor.matmul_mx(
-                out=result[t][:],
-                lhsT=wm_codes[:, t * P : (t + 1) * P].bitcast(FP8X4),
-                lhsT_scale=wm_scales[:, t * P : (t + 1) * P],
-                rhs=memory_codes[:].bitcast(FP8X4),
-                rhs_scale=memory_scales[:],
-                start=True,
-                stop=False,
-            )
 
         out_rows = by_four(out_0)
-        picked_after = ("minus_s0", "minus_s1", "vals_raw1", "vals_raw1")
-        codes_after = ("minus_s1", "vals_raw2", None, None)
+        picked_after = ("minus_s0", "memory_grouped", "vals_raw1", "vals_grouped1")
+        codes_after = ("vals_raw1", "vals_raw2", None, None)
 
         def turn_values(t):
             picked = sbuf("vals_picked%d" % t, [P, I], BF16, after=picked_after[t])
@@ -219,10 +228,9 @@ def tile_attend_largestof3_addedmemory_lean_pl_kernel(
                 stop=True,
             )
 
-        vals_grouped = [turn_values(0), turn_values(1)]
-        multiply(0, vals_grouped[0])
-        vals_grouped.append(turn_values(2))
+        vals_grouped = [turn_values(t) for t in range(PACK - 1)]
         multiply(1, vals_grouped[1])
+        multiply(0, vals_grouped[0])
         vals_grouped.append(turn_values(3))
         multiply(2, vals_grouped[2])
         finished = sbuf("finished", [P, PACK, Q], F32, after="vals_raw3")

@@ -152,7 +152,7 @@ def tile_attend_largestof3_addedmemory_lean_pl_kernel(
             vector_copy(memory_grouped[:, :, 2 * pair : 2 * pair + 2], picked[:].rearrange("p j q -> p q j"))
 
         def negated_scores(h, after):
-            larger = sbuf("larger%d" % h, [P, I], F32, after="larger")
+            larger = sbuf("larger%d" % h, [P, I], F32, after="mstore_raw1")
             nc.vector.tensor_tensor(larger[:], token_scores[h][:], page_picked[h][:], ALU.max)
             negated = sbuf("minus_s%d" % h, [P, I], F32, after=after)
             nc.vector.tensor_tensor(negated[:], page_scores[h][:].indirect(base_list[:]), larger[:], ALU.subtract)
@@ -160,7 +160,7 @@ def tile_attend_largestof3_addedmemory_lean_pl_kernel(
 
         pick_memory(0, vector_copy, "pages1_grouped")
         minus_s = [negated_scores(0, None)]
-        pick_memory(1, scalar_copy, "a_picked0")
+        pick_memory(1, scalar_copy, None)
         memory_codes, memory_scales = quantise("memory", memory_grouped[:].rearrange("p q t -> p (q t)"), Q)
         result = [scores_psum.tile([P, Q], F32, name="result%d" % t, tag="scores") for t in range(PACK)]
         for t in range(PACK):
@@ -175,8 +175,9 @@ def tile_attend_largestof3_addedmemory_lean_pl_kernel(
             )
         minus_s.append(negated_scores(1, "memory_grouped"))
         weights_grouped = sbuf("weights_grouped", [P, Q, PACK], BF16)
-        for h in range(HALVES):
-            weights = sbuf("weights%d" % h, [P, PACK, P], F32)
+
+        def turn_weights(h, after):
+            weights = sbuf("weights%d" % h, [P, PACK, P], F32, after=after)
             nc.scalar.activation(
                 weights[:].rearrange("p t s -> p s t"),
                 minus_s[h][:].rearrange("p (s t) -> p s t", t=PACK),
@@ -192,19 +193,10 @@ def tile_attend_largestof3_addedmemory_lean_pl_kernel(
                 slot_factor[:].unsqueeze(1).to_broadcast([P, P, PACK]),
                 ALU.mult,
             )
-        weight_codes, weight_scales = quantise("weights", weights_grouped[:].rearrange("p q t -> p (q t)"), Q)
-
-        out_rows = by_four(out_0)
-        picked_after = ("minus_s0", "memory_grouped", "vals_raw1", "vals_grouped1")
-        codes_after = ("vals_raw1", "vals_raw2", None, None)
 
         def turn_values(t):
-            picked = sbuf("vals_picked%d" % t, [P, I], BF16, after=picked_after[t])
-            if t < PACK - 1:
-                scalar_copy(picked[:], vals_raw[t][:].indirect(token_list[:]))
-            else:
-                vector_copy(picked[:, : I // 2], vals_raw[t][:].indirect(token_list[:, : I // 32]))
-                scalar_copy(picked[:, I // 2 :], vals_raw[t][:].indirect(token_list[:, I // 32 :]))
+            picked = sbuf("vals_picked%d" % t, [P, I], BF16)
+            scalar_copy(picked[:], vals_raw[t][:].indirect(token_list[:]))
             pairs = picked[:].bitcast(F32)
             turned = turn_psum.tile([P, PACK, P], F32, name="turned")
             for u in range(2):
@@ -215,6 +207,14 @@ def tile_attend_largestof3_addedmemory_lean_pl_kernel(
                 turned[:, 0:2, :].rearrange("p u e -> p e u"),
             )
             return grouped
+
+        turn_weights(0, "mstore_raw3")
+        vals_grouped = [turn_values(0)]
+        turn_weights(1, "vals_raw0")
+        weight_codes, weight_scales = quantise("weights", weights_grouped[:].rearrange("p q t -> p (q t)"), Q)
+
+        out_rows = by_four(out_0)
+        codes_after = ("vals_raw2", "vals_picked2", None, None)
 
         def multiply(t, grouped):
             codes, scales = quantise("vals%d" % t, grouped[:], P, after=codes_after[t])
@@ -228,9 +228,9 @@ def tile_attend_largestof3_addedmemory_lean_pl_kernel(
                 stop=True,
             )
 
-        vals_grouped = [turn_values(t) for t in range(PACK - 1)]
-        multiply(1, vals_grouped[1])
+        vals_grouped.extend([turn_values(1), turn_values(2)])
         multiply(0, vals_grouped[0])
+        multiply(1, vals_grouped[1])
         vals_grouped.append(turn_values(3))
         multiply(2, vals_grouped[2])
         finished = sbuf("finished", [P, PACK, Q], F32, after="vals_raw3")

@@ -63,6 +63,11 @@ def tile_attend_largestof3_addedmemory_lean_pl_kernel(
         def vector_copy(out, in_):
             nc.vector.tensor_copy(out=out, in_=in_)
 
+        warm_in = sbuf("warm_in", [P, 8], F32)
+        warm_out = sbuf("warm_out", [P, 8], F32)
+        nc.vector.memset(warm_in[:], 0.0)
+        nc.scalar.activation(warm_out[:], warm_in[:], ACT.Sigmoid, scale=-1.0)
+
         key_scales = sbuf("key_scales", [P, T], U8)
         nc.vector.memset(key_scales[:].bitcast(I32), 0)
         query_raw = load("query_raw", [P, PACK, Q], F32, by_four(query))

from contextlib import ExitStack

import concourse.mybir as mybir
from concourse.masks import make_identity

D, T, I, Q, E, Z, M, C = 512, 2048, 512, 256, 512, 1024, 1024, 512
FLOPS = 2 * Q * (D * T + D * Z + I * E + C * E)

F32 = mybir.dt.float32
BF16 = mybir.dt.bfloat16
I32 = mybir.dt.int32
U32 = mybir.dt.uint32
U16 = mybir.dt.uint16
U8 = mybir.dt.uint8
FP8X4 = mybir.dt.float8_e4m3fn_x4
FP4X4 = mybir.dt.float4_e2m1fn_x4
ALU = mybir.AluOpType
ACT = mybir.ActivationFunctionType

P = 128
PACK = 4
BANK = 512
HALVES = Q // P


def tile_attend_largestof3_addedmemory_lean_pl_kernel(
    tc, query, query2, keys_words, keys_scales, pages, slot_scale, vals, wm, mstore, offs, offs2, offs3, offs4, out_0, out_1, out_2
):
    nc = tc.nc
    with ExitStack() as ctx:
        keep = ctx.enter_context(tc.tile_pool(name="keep", bufs=1))
        scores_psum = ctx.enter_context(tc.psum_pool(name="scores_psum", bufs=4))
        turn_psum = ctx.enter_context(tc.psum_pool(name="turn_psum", bufs=4))

        def sbuf(name, shape, dtype, after=None):
            return keep.tile(shape, dtype, name=name, tag=after or name, align_bytes=64)

        def by_four(rows):
            return rows.rearrange("(p j) w -> p j w", j=PACK)

        def load(name, shape, dtype, source):
            tile = sbuf(name, shape, dtype)
            nc.sync.dma_start(tile[:], source)
            return tile

        def quantise(name, grouped, words, after=None):
            codes = sbuf(name + "_codes", [P, words], U32, after=after)
            scales = sbuf(name + "_scales", [P, words], U8)
            nc.vector.quantize_mx(out=codes[:].bitcast(FP8X4), scales=scales[:], in_=grouped)
            return codes, scales

        def interleave(name, raw, width):
            grouped = sbuf(name + "_grouped", [P, width * PACK], BF16)
            nc.vector.tensor_copy(
                out=grouped[:].rearrange("p (c i t) -> p c t i", i=4, t=PACK),
                in_=raw.rearrange("p t (c i) -> p c t i", i=4),
            )
            return grouped

        def scalar_copy(out, in_):
            nc.scalar.activation(out, in_, ACT.Copy)

        def vector_copy(out, in_):
            nc.vector.tensor_copy(out=out, in_=in_)

        warm_in = sbuf("warm_in", [P, 8], F32)
        warm_out = sbuf("warm_out", [P, 8], F32)
        nc.vector.memset(warm_in[:], 0.0)
        nc.scalar.activation(warm_out[:], warm_in[:], ACT.Sigmoid, scale=-1.0)

        key_scales = sbuf("key_scales", [P, T], U8)
        nc.vector.memset(key_scales[:].bitcast(I32), 0)
        query_raw = load("query_raw", [P, PACK, Q], F32, by_four(query))
        for quad in range(4):
            nc.sync.dma_start(
                key_scales[32 * quad : 32 * quad + 4, :].bitcast(I32),
                keys_scales[0, 4 * quad : 4 * quad + 4, :].bitcast(I32),
            )
        key_words = [sbuf("key_words%d" % n, [P, T], U8) for n in range(2)]
        for n in range(2):
            nc.sync.dma_start(key_words[n][:].bitcast(I32), keys_words[0, :, n * T : (n + 1) * T].bitcast(I32))
        token_list = load("token_list", [P, I // 16], U16, offs)
        query2_raw = load("query2_raw", [P, PACK, Q], F32, by_four(query2))
        pages_raw = [
            load("pages_raw%d" % n, [P, PACK, BANK], F32, by_four(pages)[:, :, n * BANK : (n + 1) * BANK])
            for n in range(Z // BANK)
        ]
        page_list = load("page_list", [P, I // 16], U16, offs2)
        base_list = load("base_list", [P, I // 16], U16, offs3)
        memory_list = load("memory_list", [P, Q // 16], U16, offs4)
        slot_factor = load("slot_factor", [P, PACK], F32, slot_scale.rearrange("o (p t) -> p (o t)", t=PACK))
        wm_raw = load("wm_raw", [P, PACK, E], F32, by_four(wm))
        mstore_raw = [load("mstore_raw%d" % j, [P, M], F32, by_four(mstore)[:, j, :]) for j in range(PACK)]
        vals_raw = [load("vals_raw%d" % j, [P, T], F32, by_four(vals)[:, j, :]) for j in range(PACK)]

        identity = sbuf("identity", [P, P], F32)
        make_identity(nc, identity[:])

        query_mx = []
        for h in range(HALVES):
            grouped = interleave("query%d" % h, query_raw[:, :, h * P : (h + 1) * P], P)
            query_mx.append(quantise("query%d" % h, grouped[:], P))
        token_scores = []
        for h in range(HALVES):
            codes, scales = query_mx[h]
            whole = sbuf("a%d" % h, [P, T], F32)
            for n in range(T // BANK):
                bank = scores_psum.tile([P, BANK], F32, name="scores", tag="scores")
                nc.tensor.matmul_mx(
                    out=bank[:],
                    lhsT=codes[:].bitcast(FP8X4),
                    lhsT_scale=scales[:],
                    rhs=key_words[n // 2][:, 2 * (n % 2) * BANK : 2 * (n % 2 + 1) * BANK].bitcast(FP4X4),
                    rhs_scale=key_scales[:, n * BANK : (n + 1) * BANK],
                    start=True,
                    stop=True,
                )
                copy = vector_copy if (4 * h + n) in (1, 3, 5) else scalar_copy
                copy(whole[:, n * BANK : (n + 1) * BANK], bank[:])
            picked = sbuf("a_picked%d" % h, [P, I], F32)
            scalar_copy(picked[:], whole[:].indirect(token_list[:]))
            token_scores.append(picked)

        query2_codes, query2_scales = quantise("query2", interleave("query2", query2_raw[:], Q)[:], Q)
        page_scores = [sbuf("h0_%d" % h, [P, Z], F32) for h in range(HALVES)]
        for n in range(Z // BANK):
            grouped = interleave("pages%d" % n, pages_raw[n][:], BANK)
            codes, scales = quantise("pages%d" % n, grouped[:], BANK)
            for h in range(HALVES):
                bank = scores_psum.tile([P, BANK], F32, name="scores", tag="scores")
                nc.tensor.matmul_mx(
                    out=bank[:],
                    lhsT=query2_codes[:, h * P : (h + 1) * P].bitcast(FP8X4),
                    lhsT_scale=query2_scales[:, h * P : (h + 1) * P],
                    rhs=codes[:].bitcast(FP8X4),
                    rhs_scale=scales[:],
                    start=True,
                    stop=True,
                )
                scalar_copy(page_scores[h][:, n * BANK : (n + 1) * BANK], bank[:])

        page_picked = [sbuf("h0_picked%d" % h, [P, I], F32) for h in range(HALVES)]
        for h in range(HALVES):
            scalar_copy(page_picked[h][:], page_scores[h][:].indirect(page_list[:]))
        wm_grouped = sbuf("wm_grouped", [P, E * PACK], BF16, after="pages1_grouped")
        nc.vector.tensor_copy(
            out=wm_grouped[:].rearrange("p (t m j) -> p m j t", t=PACK, j=PACK),
            in_=wm_raw[:].rearrange("p j (m t) -> p m j t", t=PACK),
        )
        wm_codes, wm_scales = quantise("wm", wm_grouped[:], E)
        memory_grouped = sbuf("memory_grouped", [P, Q, PACK], BF16)

        def pick_memory(pair, copy, after):
            picked = sbuf("memory_picked%d" % pair, [P, 2, Q], BF16, after=after)
            for j in range(2):
                copy(picked[:, j, :], mstore_raw[2 * pair + j][:].indirect(memory_list[:]))
            vector_copy(memory_grouped[:, :, 2 * pair : 2 * pair + 2], picked[:].rearrange("p j q -> p q j"))

        def negated_scores(h, after):
            larger = sbuf("larger%d" % h, [P, I], F32, after="mstore_raw1")
            nc.vector.tensor_tensor(larger[:], token_scores[h][:], page_picked[h][:], ALU.max)
            negated = sbuf("minus_s%d" % h, [P, I], F32, after=after)
            nc.vector.tensor_tensor(negated[:], page_scores[h][:].indirect(base_list[:]), larger[:], ALU.subtract)
            return negated

        pick_memory(0, vector_copy, "pages1_grouped")
        minus_s = [negated_scores(0, None)]
        pick_memory(1, scalar_copy, None)
        memory_codes, memory_scales = quantise("memory", memory_grouped[:].rearrange("p q t -> p (q t)"), Q)
        result = [scores_psum.tile([P, Q], F32, name="result%d" % t, tag="scores") for t in range(PACK)]
        for t in range(PACK):
            nc.tensor.matmul_mx(
                out=result[t][:],
                lhsT=wm_codes[:, t * P : (t + 1) * P].bitcast(FP8X4),
                lhsT_scale=wm_scales[:, t * P : (t + 1) * P],
                rhs=memory_codes[:].bitcast(FP8X4),
                rhs_scale=memory_scales[:],
                start=True,
                stop=False,
            )
        minus_s.append(negated_scores(1, "memory_grouped"))
        weights_grouped = sbuf("weights_grouped", [P, Q, PACK], BF16)

        def turn_weights(h, after):
            weights = sbuf("weights%d" % h, [P, PACK, P], F32, after=after)
            nc.scalar.activation(
                weights[:].rearrange("p t s -> p s t"),
                minus_s[h][:].rearrange("p (s t) -> p s t", t=PACK),
                ACT.Sigmoid,
                scale=-1.0,
            )
            turned = turn_psum.tile([P, PACK, P], F32, name="turned")
            for t in range(PACK):
                nc.tensor.transpose(turned[:, t, :], weights[:, t, :], identity[:])
            nc.vector.tensor_tensor(
                weights_grouped[:, h * P : (h + 1) * P, :],
                turned[:].rearrange("p t q -> p q t"),
                slot_factor[:].unsqueeze(1).to_broadcast([P, P, PACK]),
                ALU.mult,
            )

        def turn_values(t):
            picked = sbuf("vals_picked%d" % t, [P, I], BF16)
            scalar_copy(picked[:], vals_raw[t][:].indirect(token_list[:]))
            pairs = picked[:].bitcast(F32)
            turned = turn_psum.tile([P, PACK, P], F32, name="turned")
            for u in range(2):
                nc.tensor.transpose(turned[:, u, :], pairs[:, u::2], identity[:])
            grouped = sbuf("vals_grouped%d" % t, [P, P * PACK], BF16)
            vector_copy(
                grouped[:].bitcast(F32).rearrange("p (e u) -> p e u", u=2),
                turned[:, 0:2, :].rearrange("p u e -> p e u"),
            )
            return grouped

        turn_weights(0, "mstore_raw3")
        vals_grouped = [turn_values(0)]
        turn_weights(1, "vals_raw0")
        weight_codes, weight_scales = quantise("weights", weights_grouped[:].rearrange("p q t -> p (q t)"), Q)

        out_rows = by_four(out_0)
        codes_after = ("vals_raw2", "vals_picked2", None, None)

        def multiply(t, grouped):
            codes, scales = quantise("vals%d" % t, grouped[:], P, after=codes_after[t])
            nc.tensor.matmul_mx(
                out=result[t][:],
                lhsT=codes[:].bitcast(FP8X4),
                lhsT_scale=scales[:],
                rhs=weight_codes[:].bitcast(FP8X4),
                rhs_scale=weight_scales[:],
                start=False,
                stop=True,
            )

        vals_grouped.extend([turn_values(1), turn_values(2)])
        multiply(0, vals_grouped[0])
        multiply(1, vals_grouped[1])
        vals_grouped.append(turn_values(3))
        multiply(2, vals_grouped[2])
        finished = sbuf("finished", [P, PACK, Q], F32, after="vals_raw3")
        for t in range(PACK - 1):
            scalar_copy(finished[:, t, :], result[t][:])
        nc.sync.dma_start(out_rows[:, : PACK - 1, :], finished[:, : PACK - 1, :])
        multiply(3, vals_grouped[3])
        scalar_copy(finished[:, PACK - 1, :], result[PACK - 1][:])
        nc.scalar.dma_start(out_rows[:, PACK - 1, :], finished[:, PACK - 1, :])
        out_codes, out_scales = quantise("out", interleave("out", finished[:], Q)[:], Q)
        nc.sync.dma_start(out_1[0].rearrange("p c r -> p (c r)").bitcast(I32), out_codes[:].bitcast(I32))
        for quad in range(4):
            queue = nc.sync if quad < 2 else nc.scalar
            queue.dma_start(
                out_2[0, 4 * quad : 4 * quad + 4, :].bitcast(I32),
                out_scales[32 * quad : 32 * quad + 4, :].bitcast(I32),
            )
